import numpy as np, ml_dtypes
CORES = [2,3,42,43,82,83,122,123]
N = 8
BF = ml_dtypes.bfloat16
def gentries(a):
    return np.ascontiguousarray(a.reshape(8, 16, -1).transpose(0, 2, 1)).reshape(8, -1)
def gtable(e):
    e = np.asarray(e); return np.ascontiguousarray(e.reshape(8, -1, 16).transpose(0, 2, 1)).reshape(128, -1).astype(np.int32)
S, Q, T, CAP, RO = 2048, 2, 256, 112, 3
B = Q * S
def near(rng, c, a):
    return np.clip(np.take_along_axis(c, a[:, :, None, :], 3) + rng.integers(-40, 41, (N, 8, 16, T)), 0, 255)
def parts(rng):
    c = rng.integers(0, 256, (N, 8, 16, S)); g = rng.integers(-16, 16, (N, 8, 16, B))
    H = S >> 4; hub = np.argsort(rng.random((N, 8, S)), axis=2)[..., :H]
    i = np.minimum((H * rng.random((N, 8, 16 * S)) ** 2).astype(np.int64), H - 1)
    u = np.take_along_axis(hub, i, 2).reshape(N, 8, 16, S); u = np.where(rng.random(u.shape) < 0.5, u, rng.integers(0, S, u.shape))
    i = np.minimum((H * rng.random((N, 8, T)) ** 2).astype(np.int64), H - 1)
    a = np.take_along_axis(hub, i, 2); a = np.where(rng.random(a.shape) < 0.5, a, rng.integers(0, S, a.shape))
    h = rng.integers(0, Q, (N, 8, S)); e = rng.choice(np.array([0.1, 0.3, 0.6]), (N, 8, 1))
    f = np.where(rng.random((N, 8, S)) < e, 0, rng.integers(0, Q + 1, (N, 8, S)))
    return c, u, g, h, f, a, near(rng, c, a)
def pack(c, u, g, h, f, a, z):
    return {"xs": np.ascontiguousarray(c.reshape(N, 128, S)).astype(np.float32).astype(BF), "su": np.ascontiguousarray(u.reshape(N, 128, S)).astype(np.int32),
            "gs": np.ascontiguousarray(g.reshape(N, 128, B)).astype(np.float32).astype(BF), "hd0": h.astype(np.int32), "fl0": f.astype(np.int32),
            "a0": np.stack([gtable(v) for v in a]), "z0": np.ascontiguousarray(z.reshape(N, 128, T)).astype(np.float32).astype(BF)}
def setup_inputs(rng):
    return pack(*parts(rng))
def setup_inputs_room(rng):
    c, u, g, h, f, a, z = parts(rng); num = (CAP, CAP + 1, T, CAP - 1, 1, 0, CAP, CAP + 1)
    for r in range(N):
        for k in range(8):
            j = (r + k) % 8; o = rng.permutation(S)[:T]; a[r, k] = o
            full = rng.integers(1, Q + 1, T)
            if j in (3, 5, 6):
                full[:] = 1 if j == 5 else Q
                u[r, k] = np.arange(S)
            f[r, k, o] = np.where(rng.permutation(T) < num[j], 0, full)
    return pack(c, u, g, h, f, a, near(rng, c, a))
def setup_inputs_crowd(rng):
    c, u, g, h, f, a, z = parts(rng)
    for r in range(N):
        for k in range(8):
            j = (r + k) % 8
            if j == 7: continue
            o = np.concatenate([rng.permutation(np.array([0, S - 1])), 1 + rng.permutation(S - 2)])
            if j < 4:
                n = (1, 2, 5, 12)[j]; a[r, k] = o[rng.integers(0, n, T)]; u[r, k] = o[rng.integers(0, n, (16, S))]
            else:
                w = (Q, Q, Q + 1)[j - 4]; o = o[:(T + w - 1) // w]
                a[r, k] = rng.permutation(np.repeat(o, w)[:T]); f[r, k, o] = (Q, 0, 0)[j - 4]
    return pack(c, u, g, h, f, a, near(rng, c, a))
def setup_inputs_ties(rng):
    c, u, g, h, f, a, z = parts(rng); pro = rng.integers(2, 254, (8, 16, 3))
    for k in range(8):
        if k % 2 == 0:
            c[:, k] = pro[k][:, np.arange(S) % 3]; g[:, k] = 2 * rng.integers(0, 2, (N, 16, B)) - 1; f[:, k] = f[:, k] * (rng.random((N, S)) < 0.5)
            if k % 4 == 2:
                g[:, k] = g[:, k] * rng.integers(0, 2, (N, 1, B)); u[:, k, 0] = np.where(rng.random((N, S)) < 0.5, np.arange(S), u[:, k, 0])
        else:
            c[:, k] = c[:, k][..., np.arange(S) // 2 * 2]; g[:, k] = g[:, k][..., np.arange(B) & 31]
    z = near(rng, c, a); z[:, ::2] = np.take_along_axis(c[:, ::2], a[:, ::2, None, :], 3)
    return pack(c, u, g, h, f, a, z)
def setup_inputs_ends(rng):
    c, u, g, h, f, a, z = parts(rng)
    c = 255 * rng.integers(0, 2, c.shape); g = 31 * rng.integers(0, 2, g.shape) - 16; z = 255 * rng.integers(0, 2, z.shape)
    k = rng.integers(0, 3, (N, 8, 1, T)); z = np.where(k == 0, 0, np.where(k == 1, 255, z))
    p = rng.permutation(8)
    f[:, p[0]] = 0; f[:, p[1]] = Q; h[:, p[2]] = Q - 1; h[:, p[3]] = 0
    for j in (4, 5, 6):
        w = p[j]; cw = rng.integers(0, 2, (N, 16, S)); zw = 255 - rng.integers(0, 2, (N, 16, T)); f[:, w] = Q * rng.integers(0, 2, (N, S))
        if j < 6:
            two = np.argsort(rng.random((N, 16, B)), axis=1) < 2
            gw = np.where(two, -rng.integers(1, 9, (N, 16, B)), rng.integers(6, 16, (N, 16, B)))
            if j == 5: cw = 255 - cw; zw = 255 - zw; gw = -gw
            g[:, w] = gw
        c[:, w] = cw; z[:, w] = zw
    a[..., 0] = 0; a[..., 1] = S - 1; a[..., T - 2] = 0; a[..., T - 1] = S - 1
    u = np.where(rng.random(u.shape) < 0.3, (S - 1) * rng.integers(0, 2, u.shape), u)
    return pack(c, u, g, h, f, a, z)
def setup_inputs_spread(rng):
    c, u, g, h, f, a, z = parts(rng)
    c = np.minimum((256 * rng.random(c.shape) ** np.exp2(rng.uniform(-3, 3, (N, 8, 1, S)))).astype(np.int64), 255)
    z = np.minimum((256 * rng.random(z.shape) ** np.exp2(rng.uniform(-3, 3, (N, 8, 1, T)))).astype(np.int64), 255)
    g = np.clip(np.floor((rng.random(g.shape) * 2 - 1) * np.exp2(rng.uniform(-2, 4, (N, 8, 1, B)))).astype(np.int64), -16, 15)
    m = rng.permuted(np.tile(np.arange(S), (N, 8, 1)), axis=2)
    i = np.minimum((S * rng.random((N, 8, 16 * S)) ** rng.uniform(1, 5, (N, 8, 1))).astype(np.int64), S - 1); u = np.take_along_axis(m, i, 2).reshape(N, 8, 16, S)
    i = np.minimum((S * rng.random((N, 8, T)) ** rng.uniform(1, 5, (N, 8, 1))).astype(np.int64), S - 1); a = np.take_along_axis(m, i, 2)
    f = np.minimum(((Q + 1) * rng.random((N, 8, S)) ** np.exp2(rng.uniform(-2, 2, (N, 8, 1)))).astype(np.int64), Q)
    return pack(c, u, g, h, f, a, z)
def check_inputs(d):
    bad = []
    for k, lo, hi in (("xs", 0, 255), ("su", 0, S - 1), ("gs", -16, 15), ("hd0", 0, Q - 1), ("fl0", 0, Q), ("a0", 0, S - 1), ("z0", 0, 255)):
        v = np.asarray(d[k]).astype(np.float64)
        if not (np.all(v >= lo) and np.all(v <= hi) and np.all(v == np.floor(v))): bad.append("range of " + k)
    return bad
def reference(xs, su, gs, hd0, fl0, a0, z0):
    X = xs.astype(np.float32).astype(np.int64).reshape(N, 8, 16, S); U = su.astype(np.int64).reshape(N, 8, 16, S)
    G = gs.astype(np.float32).astype(np.int64).reshape(N, 8, 16, B); hd = hd0.astype(np.int64); fl = fl0.astype(np.int64)
    a = np.stack([gentries(v) for v in a0]).astype(np.int64); z = z0.astype(np.float32).astype(np.int64).reshape(N, 8, 16, T)
    low = np.tri(T, k=-1, dtype=bool); odd = 2 * np.arange(16)[:, None] + 1
    for t in range(RO):
        same = a[:, :, :, None] == a[:, :, None, :]
        place = np.sum(same & low, axis=3); count = np.sum(same, axis=3)
        ha = np.take_along_axis(hd, a, 2); fa = np.take_along_axis(fl, a, 2)
        pop = place < fa; slot = Q * a + ((ha + place) & (Q - 1))
        zn = np.clip(z + np.take_along_axis(G, slot[:, :, None, :], 3), 0, 255)
        s = np.take_along_axis(U, a[:, :, None, :], 3)
        c = np.take_along_axis(X, s.reshape(N, 8, 1, 16 * T), 3).reshape(N, 8, 16, 16, T)
        best = np.argmin(np.sum(np.abs(c - zn[:, :, :, None, :]), axis=2), axis=2)
        to = np.take_along_axis(s, best[:, :, None, :], 2)[:, :, 0]
        gone = np.minimum(count, fa)
        np.put_along_axis(hd, a, (ha + gone) & (Q - 1), 2); np.put_along_axis(fl, a, fa - gone, 2)
        ask = ~pop & (np.add.accumulate((~pop).astype(np.int64), axis=2) <= CAP)
        d = 1 + t % (N - 1); XR = np.roll(X, -d, axis=0); GR = np.roll(G, -d, axis=0)
        u = np.sum(odd * z, axis=2) & 4095
        ix = (((u * u) >> 5)[:, :, None, :] + odd * u[:, :, None, :]) & (B - 1)
        cand = np.take_along_axis(GR, ix.reshape(N, 8, 1, 16 * T), 3).reshape(N, 8, 16, 16, T)
        goal = np.take_along_axis(XR, a[:, :, None, :], 3)
        m = np.argmin(np.sum(np.abs(z[:, :, :, None, :] + cand - goal[:, :, :, None, :]), axis=2), axis=2)
        seg = np.take_along_axis(cand, m[:, :, None, None, :], 3)[:, :, :, 0]
        put = ask & (place - fa < Q)
        for r in range(N):
            for g in range(8):
                w = np.flatnonzero(put[r, g])
                G[r, g][:, slot[r, g, w]] = seg[r, g][:, w]
                np.add.at(fl[r, g], a[r, g, w], 1)
        a = np.where(pop, to, a); z = np.where(pop[:, :, None, :], zn, z)
    return {"yz": z.reshape(N, 128, T).astype(np.float32).astype(BF), "ya": a.astype(np.float32), "yh": hd.astype(np.float32), "yf": fl.astype(np.float32)}

@@ -1,0 +1,528 @@
+from concourse.bass import DstId, RemoteDMATransfer
+from concourse.mybir import AluOpType as A, ActivationFunctionType as F
+
+SCRATCH = {}
+
+
+def _b(n, c, d="bfloat16", w="sbuf", p=128):
+    SCRATCH[n] = (w, [p, c], d)
+
+
+for _n, _c in (("X", 2048), ("G", 4368), ("FB", 128), ("HB", 128), ("cS", 4096), ("cA", 4096), ("AB", 4096), ("AC", 4096),
+               ("E", 4096), ("mI", 128), ("mNI", 128), ("SG", 128), ("SGf", 128), ("SGh", 128), ("SGp", 128), ("ZE", 144),
+               ("ZW", 144), ("ZL", 144), ("ZA", 144), ("TRI", 128), ("Fa", 2048), ("Ff", 2048), ("Fh", 2048), ("LTm", 2048),
+               ("WR1", 128), ("WR2", 128), ("REP", 512), ("KBS", 48), ("KBA", 24), ("PH", 256), ("PL", 256), ("ONE", 128),
+               ("CRS", 512), ("CRA", 256), ("ZROW", 256), ("RR", 512), ("blB", 16), ("scB", 16), ("hpB", 16), ("fpB", 16),
+               ("vhB", 16), ("vlB", 16), ("shB", 256), ("slB", 256), ("zt", 256), ("WTS", 256), ("WTA", 256), ("goal", 256),
+               ("PB", 48), ("T16", 512), ("Z0", 256), ("Z1", 256), ("Z2", 256), ("Z3", 256), ("AN0", 256), ("AN1", 256),
+               ("LN0", 256), ("LN1", 256), ("QZ0", 256), ("QZ1", 256)):
+    _b(_n, _c)
+for _n, _c in (("HF", 2304), ("JX", 144), ("JG", 128), ("JM", 128), ("JPH", 256), ("JPL", 256), ("JR", 512), ("RA", 128),
+               ("RB", 128), ("J16", 16), ("KB2", 16), ("COL", 128), ("OH", 16), ("LT", 16), ("LA", 48), ("W1", 128),
+               ("ZR16", 16), ("LL", 512), ("KU", 256), ("K1", 256), ("K2", 128), ("K3", 64), ("HV", 256),
+               ("aF0", 48), ("aF1", 48), ("aF2", 48), ("aF3", 48), ("UV0", 32), ("UV1", 32), ("QU0", 32), ("QU1", 32)):
+    _b(_n, _c, "float32")
+for _n, _c in (("SU", 2048), ("IOT", 2048), ("FI", 128), ("HI", 128), ("aI", 16), ("CI", 8), ("LI", 320), ("TI", 256), ("TJ", 256),
+               ("sI", 256), ("sJ", 512), ("KI", 48), ("KJ", 48)):
+    _b(_n, _c, "int32")
+for _n, _c in (("aU0", 16), ("aU1", 16), ("aU2", 16), ("aU3", 16), ("AR", 256), ("sU", 256), ("gU", 16), ("nU", 48),
+               ("qU", 16), ("CL0", 256), ("CL1", 256), ("QC0", 256), ("QC1", 256), ("QA0", 16), ("QA1", 16)):
+    _b(_n, _c, "uint16")
+for _n in ("D0", "D1", "D2", "KEY", "PLB", "ML", "WTP", "TR"):
+    _b(_n, 512, "float32", "psum")
+SEMAPHORES = ["eV", "eS", "eP", "eG", "sent", "l_a", "l_z", "l_h", "l_f", "l_s", "l_x", "l_g", "o_z", "o_a", "o_h", "o_f",
+              "r_z0", "r_z1", "r_c0", "r_c1", "r_u0", "r_u1", "r_a0", "r_a1", "r_n0", "r_n1"]
+STEPS = 3
+
+
+def rank_program(g, core, T, topo):
+    rank = T.rank_of(core)
+    if rank is None:
+        return
+    n = len(T.cores)
+    H = {"V": g.vector, "S": g.scalar, "P": g.tensor, "G": g, "Y": g.sync}
+    cnt = {"V": 0, "S": 0, "P": 0, "G": 0}
+    known = {q: {} for q in H}
+    wr, rd, pacc = {}, {}, {}
+
+    def v(name, c0=0, c1=None, st=1, p0=0, p1=None):
+        sh = SCRATCH[name][1]
+        return (name, c0, sh[1] if c1 is None else c1, st, p0, sh[0] if p1 is None else p1)
+
+    def ap(x):
+        if not isinstance(x, tuple):
+            return x
+        if x[0] == "ind":
+            return ap(x[1]).indirect(ap(x[2]))
+        name, c0, c1, st, p0, p1 = x
+        return T[name][p0:p1, c0:c1] if st == 1 else T[name][p0:p1, c0:c1:st]
+
+    def ind(win, off):
+        return ("ind", win, off)
+
+    def wait(q, rec):
+        sem, val, kn = rec[1], rec[2], rec[3]
+        if known[q].get(sem, 0) >= val:
+            return
+        H[q].wait_ge(T.sem[sem], val)
+        for s, x in list(kn.items()) + [(sem, val)]:
+            if known[q].get(s, 0) < x:
+                known[q][s] = x
+
+    def flat(xs):
+        out = []
+        for x in xs:
+            if isinstance(x, tuple):
+                out += [x[1], x[2]] if x[0] == "ind" else [x]
+        return out
+
+    def deps(q, ws, rs):
+        need = []
+        for x in ws + rs:
+            if SCRATCH[x[0]][0] == "psum":
+                need += [r for k, r in pacc.get(x[0], {}).items() if k != q]
+            need += [r for lo, hi, r in wr.get(x[0], []) if lo < x[2] and x[1] < hi]
+        for x in ws:
+            need += [r for lo, hi, r in rd.get(x[0], []) if lo < x[2] and x[1] < hi]
+        for r in sorted(need, key=lambda r: -r[2]):
+            wait(q, r)
+
+    def note(rec, ws, rs, cover=True):
+        for x in ws + rs:
+            if SCRATCH[x[0]][0] == "psum":
+                pacc.setdefault(x[0], {})[rec[0]] = rec
+        for x in ws:
+            if SCRATCH[x[0]][0] == "psum":
+                continue
+            if x[3] == 1 and cover:
+                wr[x[0]] = [e for e in wr.get(x[0], []) if not (x[1] <= e[0] and e[1] <= x[2])]
+                rd[x[0]] = [e for e in rd.get(x[0], []) if not (x[1] <= e[0] and e[1] <= x[2])]
+            wr.setdefault(x[0], []).append((x[1], x[2], rec))
+        for x in rs:
+            if SCRATCH[x[0]][0] != "psum":
+                rd[x[0]] = [e for e in rd.get(x[0], []) if not (e[2][0] == rec[0] and not e[2][4] and x[1] <= e[0] and e[1] <= x[2])]
+                rd[x[0]].append((x[1], x[2], rec))
+
+    def op(q, call, out, *ins):
+        ws, rs = flat([out]), flat(ins)
+        if out[0] == "ind":
+            ws, rs = [out[1]], rs + [out[2]]
+        deps(q, ws, rs)
+        cnt[q] += 1
+        call().then_inc(T.sem["e" + q], 1)
+        note((q, "e" + q, cnt[q], dict(known[q]), False), ws, rs, out[0] != "ind")
+
+    def vcopy(out, in_):
+        op("V", lambda: g.vector.tensor_copy(out=ap(out), in_=ap(in_)), out, in_)
+
+    def tt(out, a, b, o):
+        op("V", lambda: g.vector.tensor_tensor(out=ap(out), in0=ap(a), in1=ap(b), op=o), out, a, b)
+
+    def ts(out, a, s1, o1, s2=None, o2=None):
+        if o2 is None:
+            op("V", lambda: g.vector.tensor_scalar(out=ap(out), in0=ap(a), scalar1=ap(s1), scalar2=None, op0=o1), out, a, s1)
+        else:
+            op("V", lambda: g.vector.tensor_scalar(out=ap(out), in0=ap(a), scalar1=ap(s1), scalar2=ap(s2), op0=o1, op1=o2), out, a, s1, s2)
+
+    def act(out, in_, f=F.Copy, scale=1.0):
+        op("S", lambda: g.scalar.activation(out=ap(out), in_=ap(in_), func=f, scale=ap(scale)), out, in_, scale)
+
+    def mm(out, lhsT, rhs, start, stop):
+        op("P", lambda: g.tensor.matmul(ap(out), ap(lhsT), ap(rhs), start, stop), out, lhsT, rhs)
+
+    def iota(out, pat, base=0, mult=0):
+        op("G", lambda: g.iota(ap(out), pat, base, mult, allow_small_or_imprecise_dtypes=True), out)
+
+    def fill(out, x):
+        op("V", lambda: g.vector.memset(ap(out), x), out)
+
+    def load(q, out, in_, sem):
+        H[q].dma_start(out=ap(out), in_=in_).then_inc(T.sem[sem], 16)
+        note((q, sem, 16, {}, True), [out], [])
+
+    final, sent = [], [0]
+
+    def store(out, in_, sem, row=None):
+        deps("Y", [], [in_])
+        src = ap(in_) if row is None else T[in_[0]][row:128:16, in_[1]:in_[2]]
+        g.sync.dma_start(out=out, in_=src).then_inc(T.sem[sem], 16)
+        final.append((sem, 16))
+
+    def send(dst, parts):
+        to = T.cores[dst]
+        rid, pid = topo.addr(to)[0], topo.addr(to)[1]
+        e = topo.engines(core, to)[:8]
+        deps("G", [], [p[0] for p in parts])
+        m = [sum(1 << x for x in e[k::len(parts)]) for k in range(len(parts))]
+        sent[0] += len(e)
+        if len(parts) == 1:
+            s, d, sem = parts[0]
+            g.remote_dma(ap(v(d)), ap(s), T.sem[sem], T.sem.sent, pid, rid, m[0])
+        else:
+            g.remote_dma_fused([RemoteDMATransfer(dst_ids=[DstId(rid=rid, pnc=pid)], dma_engine_mask=m[k], remote_sem=T.sem[sem],
+                                                  src=ap(s), dst=ap(v(d))) for k, (s, d, sem) in enumerate(parts)], local_sem=T.sem.sent)
+
+    def arrive(buf, sem, src, parts):
+        e = len(topo.engines(T.cores[src], core)[:8]) // parts
+        wr[buf] = [(0, SCRATCH[buf][1][1], ("R", sem, e, {}, True))]
+
+    load("Y", v("aI"), T.a0[:, :], "l_a")
+    load("S", v("Z0"), T.z0[:, :], "l_z")
+    load("Y", v("SU"), T.su[:, :], "l_s")
+    load("S", v("HI"), T.hd0[:, :], "l_h")
+    load("S", v("FI"), T.fl0[:, :], "l_f")
+    load("Y", v("X"), T.xs[:, :], "l_x")
+    load("S", v("G", 0, 4096), T.gs[:, :], "l_g")
+    for t in range(2):
+        p, q = (rank - 1 - t) % n, (rank + 1 + t) % n
+        for b, c in (("QZ", 2), ("QC", 2), ("QU", 1), ("QA", 1)):
+            arrive(b + str(t), "r_" + b[1].lower() + str(t), p, c)
+        arrive("LN%d" % t, "r_n%d" % t, q, 1)
+
+    iota(v("CI", 0, 1), [[0, 1]], 0, 1)
+    iota(v("JX"), [[1, 144]])
+    iota(v("J16"), [[1, 16]])
+    iota(v("JG"), [[1, 8], [0, 16]])
+    iota(v("RA"), [[0, 8], [8, 4], [0, 4]])
+    iota(v("RB"), [[0, 32], [2, 4]], 1)
+    iota(v("IOT"), [[1, 2048]])
+    iota(v("JR"), [[1, 32], [0, 16]])
+    iota(v("KB2"), [[0, 2], [1, 8]])
+    iota(v("CRA", p0=0, p1=1), [[1, 16], [0, 16]])
+    iota(v("CRS", p0=0, p1=1), [[64, 16], [0, 32]])
+    iota(v("JPH"), [[1, 16], [1000, 2], [16, 8]])
+    iota(v("JPL"), [[1, 16], [1000, 2], [16, 8]], -1000)
+
+    def col(k):
+        return v("COL", 4 * k, 4 * k + 1)
+    (pF, pm, pg, g0, g1, g15, wi, wE, c1, p8, p31, w8) = [col(k) for k in range(12)]
+
+    def cands(t, part):
+        z = "Z%d" % t
+        uv = "UV%d" % t
+        o = v("ML", 96, 112)
+        li = [v("LI", 16 * k, 16 * k + 16) for k in range(8)]
+        if part == 0:
+            for i in range(16):
+                mm(o, v("ZW", 15 - i, 143 - i), v(z, i, 256, 16), i == 0, i == 15)
+        if part == 1:
+            vcopy(li[0], o)
+            ts(li[1], li[0], 4095, A.bitwise_and)
+            tt(li[2], li[1], li[1], A.mult)
+            ts(li[3], li[2], 5, A.logical_shift_right)
+            ts(li[4], li[3], 4095, A.bitwise_and)
+            ts(li[5], li[4], 6, A.logical_shift_right)
+            ts(li[6], li[4], 63, A.bitwise_and)
+            ts(v("vhB"), li[5], 64.0, A.mult)
+            vcopy(v("vlB"), li[6])
+            r = "TR"
+            mm(v(r, 0, 256), v("WR1"), v(z), True, False)
+            mm(v(r, 0, 256), v("WR2"), v(z), False, False)
+            for i in range(16):
+                for b in ("vhB", "vlB"):
+                    mm(v(r, i, 256, 16), v("Fa", 128 * i, 128 * i + 128), v(b), False, i == 15 and b == "vlB")
+        if part == 2:
+            vcopy(v("TI"), v("TR", 0, 256))
+            ts(v("TJ"), v("TI"), 4095, A.bitwise_and)
+            vcopy(v("CL%d" % t), v("TJ"))
+            q = (rank + 1 + t) % n
+            send(q, [(v(z), "QZ%d" % t, "r_z%d" % t), (v("CL%d" % t), "QC%d" % t, "r_c%d" % t)])
+            vcopy(v(uv, 0, 16), li[1])
+            vcopy(v(uv, 16, 32), li[4])
+            send(q, [(v(uv), "QU%d" % t, "r_u%d" % t)])
+
+    def ask(t):
+        send((rank + 1 + t) % n, [(v("aU%d" % t), "QA%d" % t, "r_a%d" % t)])
+
+    vcopy(pF, v("CI", 0, 1))
+    for j, (out, o, s) in enumerate(((pm, A.bitwise_and, 15), (pg, A.logical_shift_right, 4), (p8, A.bitwise_and, 7),
+                                     (p31, A.bitwise_and, 31))):
+        ts(v("CI", 1 + j, 2 + j), v("CI", 0, 1), s, o)
+        vcopy(out, v("CI", 1 + j, 2 + j))
+    ts(g15, pg, 16.0, A.mult, 15.0, A.add)
+    ts(wi, pm, 2.0, A.mult, 1.0, A.add)
+    ts(v("ZW"), v("JX"), g15, A.is_equal, wi, A.mult)
+    vcopy(v("aU0"), v("aI"))
+    ask(0)
+    cands(0, 0)
+    ts(v("SG"), v("JG"), pg, A.is_equal)
+    ts(v("OH"), v("J16"), pm, A.is_equal)
+    for r, w in (("RA", "WR1"), ("RB", "WR2")):
+        ts(v("W1"), v(r), wi, A.mult)
+        tt(v(w), v("W1"), v("SG"), A.mult)
+    for i in range(16):
+        ts(v("Fa", 128 * i, 128 * i + 128), v("SG"), v("OH", i, i + 1), A.mult)
+    cands(0, 1)
+    ts(g0, pg, 16.0, A.mult)
+    ts(g1, g0, 1.0, A.add)
+    ts(v("SGf"), v("JX", 0, 128), g0, A.is_equal)
+    ts(v("SGh"), v("JX", 0, 128), g1, A.is_equal)
+    for i in range(16):
+        act(v("Ff", 128 * i, 128 * i + 128), v("SGf"), scale=v("OH", i, i + 1))
+        act(v("Fh", 128 * i, 128 * i + 128), v("SGh"), scale=v("OH", i, i + 1))
+    cands(0, 2)
+    vcopy(v("HB"), v("HI"))
+    vcopy(v("FB"), v("FI"))
+    for b in range(4):
+        d = "D%d" % (b % 3)
+        for k in range(4):
+            i = 4 * b + k
+            mm(v(d, 128 * k, 128 * k + 128), v("Ff", 128 * i, 128 * i + 128), v("FB"), True, False)
+            mm(v(d, 128 * k, 128 * k + 128), v("Fh", 128 * i, 128 * i + 128), v("HB"), False, True)
+        act(v("HF", 512 * b, 512 * b + 512), v(d))
+    vcopy(v("aF0", 16, 32), v("aI"))
+    vcopy(v("aF0", 32, 48), v("aI"))
+    fill(v("ONE"), 1.0)
+    fill(v("ZROW"), 0.0)
+    fill(v("ZR16"), 0.0)
+    fill(v("G", 4096, 4112), 0.0)
+    ts(v("LT"), v("J16"), pm, A.is_gt)
+    tt(v("SGp"), v("SGf"), v("SGh"), A.add)
+
+    def late_constants():
+        for i in range(1, 16):
+            ts(v("LTm", 128 * i, 128 * i + 128), v("SGf"), v("LT", i, i + 1), A.mult)
+        ts(wE, pm, 0.0, A.is_equal)
+        ts(c1, pm, 1.0, A.is_equal, 512.0, A.mult)
+        tt(wE, wE, c1, A.add)
+        ts(v("ZE"), v("JX"), g15, A.is_equal, wE, A.mult)
+        ts(v("mI"), v("JX", 0, 128), pF, A.is_equal)
+        ts(v("mNI"), v("mI"), -1.0, A.mult)
+        ts(v("REP"), v("JR"), p31, A.is_equal)
+        ts(v("JM"), v("JG"), -16.0, A.mult)
+        tt(v("JM"), v("JM"), v("JX", 0, 128), A.add)
+        ts(v("W1"), v("JM"), pm, A.is_gt)
+        tt(v("TRI"), v("W1"), v("SG"), A.mult)
+        tt(v("TRI"), v("TRI"), v("SG"), A.subtract)
+        ts(v("LA", 0, 16), v("J16"), 16.0, A.mult, 4112.0, A.add)
+        ts(v("LA", 0, 16), v("LA", 0, 16), pm, A.add)
+        ts(v("LA", 16, 32), v("LA", 0, 16), -2064.0, A.add)
+        ts(v("LA", 32, 48), v("LA", 0, 16), -2064.0, A.add)
+        for k, f in enumerate((1.0, 2.0, -1.0)):
+            ts(v("KBA", 8 * k, 8 * k + 8), v("KB2", 0, 8), pg, A.is_equal, 16.0 * f, A.mult)
+            ts(v("KBS", 16 * k, 16 * k + 16), v("KB2"), pg, A.is_equal, 1024.0 * f, A.mult)
+        ts(c1, p8, 16.0, A.mult, 15.0, A.add)
+        ts(v("ZA"), v("JX"), c1, A.is_equal)
+        ts(w8, pF, 8.0, A.is_lt, 63.0, A.mult)
+        ts(w8, w8, 1.0, A.add)
+        ts(v("ZL"), v("ZA"), w8, A.mult)
+        ts(v("PH"), v("JPH"), pF, A.is_equal)
+        ts(v("PL"), v("JPL"), pF, A.is_equal)
+
+    def gather(q, out, k0, k1, win, lst):
+        o, i = v(out, 512 * k0, 512 * k1), ind(win, v(lst, 32 * k0, 32 * k1))
+        vcopy(o, i) if q == "V" else act(o, i)
+
+    def terms(bank, pos, neg):
+        for h in range(2):
+            o, s = v(bank, 128 * h, 128 * h + 128), (128 * h, 128 * h + 128)
+            mm(o, v(pos, *s), v("mI"), True, not neg)
+            if neg:
+                mm(o, v(neg, *s), v("mNI"), False, True)
+
+    def dist(ab, src, term, order):
+        for k in order:
+            h, r = k // 4, 32 * (k % 4)
+            d = v(("D0", "D1")[k % 2] if h == 0 else ("D2", "WTP")[k % 2])
+            s, o = v(src, 512 * k, 512 * k + 512), v(ab, 512 * k, 512 * k + 512)
+            if h == 0:
+                mm(d, v("mNI"), s, True, False)
+            mm(d, v(term, 128 * h, 128 * h + 128, 1, r, r + 32), v("REP", p0=r, p1=r + 32), h == 1, True)
+            if h == 0:
+                act(o, d, F.Abs)
+            else:
+                tt(o, s, d, A.max)
+
+    def sums(bank, src, h, kb, k, w, last):
+        for m in range(16):
+            mm(v(bank, m * 2 * w + h, (m + 1) * 2 * w, 2), v(src, m + 2048 * h, 2048 * h + 2048, 16), v(kb, k * w, k * w + w), False,
+               last and m == 15)
+
+    def least(bank, w, k0):
+        u = 16 * w
+        vcopy(v("KU", 0, u), v(bank, u, 2 * u))
+        tt(v("K1", 0, u), v(bank, 0, u), v("KU", 0, u), A.min)
+        tt(v("K2", 0, u // 2), v("K1", 0, u // 2), v("K1", u // 2, u), A.min)
+        tt(v("K3", 0, u // 4), v("K2", 0, u // 4), v("K2", u // 4, u // 2), A.min)
+        tt(v("KI", k0, k0 + u // 8), v("K3", 0, u // 8), v("K3", u // 8, u // 4), A.min)
+
+    def turn(w, mask, k0, bank):
+        ts(v("KJ", k0, k0 + 2 * w), v("KI", k0, k0 + 2 * w), mask, A.bitwise_and)
+        vcopy(v("PB", k0, k0 + 2 * w), v("KJ", k0, k0 + 2 * w))
+        for h in range(2):
+            mm(v(bank, 256 + 128 * h, 384 + 128 * h, 1, 0, w), v("PB", k0 + h, k0 + 2 * w, 2), v("mI"), True, True)
+
+    def row(w, k0, bank):
+        vcopy(v("T16", 8 * k0, 8 * k0 + 256, 1, 0, w), v(bank, 256, 512, 1, 0, w))
+
+    def lists(w, k0, zs, o):
+        for i in range(16):
+            mm(o, v(zs, 15 - i, 143 - i, 1, 0, w), v("T16", 8 * k0 + i, 8 * k0 + 256, 16, 0, w), i == 0, i == 15)
+
+    for t in range(STEPS):
+        last = t == STEPS - 1
+        aF, aU, z, zn = "aF%d" % t, v("aU%d" % t), "Z%d" % t, "Z%d" % (t + 1)
+        aL, slot = v(aF, 16, 32), v(aF, 0, 16)
+        nn, ss, t1, segf, ask_, q1, n0, lf, pop, fm, ak, put, wA, n1 = [v("LL", 16 * x, 16 * x + 16) for x in range(14)]
+        three, t2 = v("LL", 176, 224), v("LL", 240, 256)
+        k, f, ct, hh, hs, hk = [v("LI", x, x + 16) for x in (224, 240, 256, 272, 128, 144)]
+        o, ro, mo, so = v("ML", 0, 32), v("ML", 64, 80), v("ML", 160, 176), v("ML", 128, 144)
+
+        def keys():
+            mm(v("KEY"), v("ONE", p0=0, p1=1), v("CRS", p0=0, p1=1), True, False)
+            for h in range(2):
+                for b, w in (("shB", "PH"), ("slB", "PL")):
+                    mm(v("KEY", h, 512, 2), v(b, 128 * h, 128 * h + 128), v(w), False, False)
+            sums("KEY", "cS", 1, "KBS", 2, 16, False)
+
+        def decide():
+            ts(ask_, ro, 112.0, A.is_lt)
+            ts(pop, v("blB"), -1.0, A.mult, 1.0, A.add)
+            ts(q1, nn, 1.0, A.is_le)
+            ts(t1, nn, 1.0, A.add)
+            ts(n0, nn, 0.0, A.is_equal)
+            tt(ask_, ask_, v("blB"), A.mult)
+            ts(t2, nn, -1.0, A.mult, -1.0, A.add)
+            tt(lf, ct, k, A.subtract)
+            tt(fm, t1, ask_, A.mult)
+            tt(v("hpB"), n0, hk, A.is_equal)
+            tt(v("fpB"), t2, fm, A.max)
+            ts(lf, lf, 1.0, A.is_equal)
+            tt(put, q1, ask_, A.mult)
+            ts(n1, nn, 1.0, A.is_equal)
+            tt(lf, lf, pop, A.mult)
+            tt(ak, aL, v("blB"), A.mult)
+            tt(wA, n0, lf, A.max)
+            tt(n1, n1, ask_, A.mult)
+            ts(three, three, -1.0, A.mult, 1.0, A.add)
+            tt(three, three, v("LA"), A.mult)
+            tt(three, three, v(aF), A.max)
+            vcopy(v("nU"), three)
+
+        def values():
+            for i in range(16):
+                mm(v("TR", i, 256, 16), v("Ff", 128 * i, 128 * i + 128), v("fpB"), True, False)
+                mm(v("TR", i, 256, 16), v("Fh", 128 * i, 128 * i + 128), v("hpB"), False, True)
+            act(v("HV"), v("TR", 0, 256))
+
+        vcopy(v("AR"), ind(v("IOT"), aU))
+        vcopy(v("sI"), ind(v("SU"), aU))
+        vcopy(v("sU"), v("sI"))
+        if t:
+            vcopy(v("AN%d" % (t - 1)), ind(v("G", 0, 4096), v("qU")))
+            send((rank - t) % n, [(v("AN%d" % (t - 1)), "LN%d" % (t - 1), "r_n%d" % (t - 1))])
+        gather("S", "cS", 0, 2, v("X"), "sU")
+        mm(v("PLB", 0, 256), v("ONE", p0=0, p1=1), v("ZROW", p0=0, p1=1), True, False)
+        for c in range(16):
+            e = 256 * c
+            ts(v("E", e, e + 256), v("AR"), v(aF, 16 + c, 17 + c), A.is_equal)
+            mm(v("PLB", 0, 16 * c + 16), v("SGh"), v("E", e, e + 16 * c + 16), False, False)
+            if c < 15:
+                mm(v("PLB", 16 * c + 16, 256), v("SGp"), v("E", e + 16 * c + 16, e + 256), False, False)
+        if t == 0:
+            late_constants()
+        for i in range(1, 16):
+            mm(v("PLB", i, 256, 16), v("LTm", 128 * i, 128 * i + 128), v("E", i, 4096, 272), False, i == 15)
+        act(v("RR", 0, 256), v("PLB", 0, 256))
+        if t:
+            vcopy(ind(v("HF"), v("nU", 32, 48)), v("HV"))
+        act(v("RR", 256, 512), ind(v("HF", 0, 2048), aU))
+        for i in range(16):
+            mm(o, v("ZE", 15 - i, 143 - i), v("RR", i, 512, 16), i == 0, i == 15)
+        if t:
+            vcopy(ind(v("G"), v("nU", 0, 16)), v("LN%d" % (t - 1)))
+        if last:
+            gather("V", "cS", 6, 8, v("X"), "sU")
+            gather("S", "cS", 2, 6, v("X"), "sU")
+        else:
+            gather("V", "cA", 4, 6, v("G", 0, 4096), "QC%d" % t)
+            act(v("goal"), ind(v("X"), v("QA%d" % t)))
+            gather("S", "cA", 0, 4, v("G", 0, 4096), "QC%d" % t)
+            terms("WTP", "goal", "QZ%d" % t)
+            gather("S", "cA", 6, 8, v("G", 0, 4096), "QC%d" % t)
+        vcopy(v("LI", 192, 224), o)
+        ts(v("LI", 224, 256), v("LI", 192, 224), 511, A.bitwise_and)
+        ts(v("LI", 256, 288), v("LI", 192, 224), 9, A.logical_shift_right)
+        tt(nn, k, f, A.subtract)
+        tt(hs, hh, k, A.add)
+        ts(v("blB"), nn, 0.0, A.is_ge)
+        ts(hk, hs, 1, A.bitwise_and)
+        ts(ss, aL, 2.0, A.mult)
+        ts(t1, v("blB"), 4096.0, A.mult)
+        tt(slot, ss, hk, A.add)
+        tt(segf, t1, slot, A.max)
+        vcopy(v("gU"), segf)
+        tt(v("zt"), ind(v("G", 0, 4112), v("gU")), v(z), A.add)
+        ts(v(zn), v("zt"), 0.0, A.max, 255.0, A.min)
+        if not last:
+            ts(v("WTA"), v("WTP", 0, 256), -16.0, A.max, 16.0, A.min)
+        op("V", lambda: g.vector.tensor_tensor_scan(out=ap(v("scB")), data0=ap(v("blB")), data1=ap(v("ZR16")), initial=0.0, op0=A.add, op1=A.add),
+           v("scB"), v("blB"), v("ZR16"))
+        terms("TR", zn, None)
+        vcopy(v("WTS"), v("TR", 0, 256))
+        ts(v("sJ", 0, 256), v("sI"), 6, A.logical_shift_right)
+        ts(v("sJ", 256, 512), v("sI"), 63, A.bitwise_and)
+        vcopy(v("shB"), v("sJ", 0, 256))
+        vcopy(v("slB"), v("sJ", 256, 512))
+        mm(ro, v("SG"), v("scB"), True, False)
+        mm(ro, v("TRI"), v("blB"), False, True)
+        if last:
+            store(T.yz[:, :], v(zn), "o_z")
+            decide()
+            dist("AB", "cS", "WTS", (4, 5, 0, 1, 2, 3, 6, 7))
+            values()
+            keys()
+        else:
+            mm(v("PLB", 0, 256), v("ONE", p0=0, p1=1), v("CRA", p0=0, p1=1), True, False)
+            dist("AC", "cA", "WTA", (4, 0, 5, 1, 6, 2, 7, 3))
+            sums("PLB", "cA", 1, "KBA", 2, 8, False)
+            sums("PLB", "AC", 0, "KBA", 0, 8, False)
+            sums("PLB", "AC", 1, "KBA", 1, 8, True)
+            gather("S", "cS", 4, 6, v("X"), "sU")
+            gather("S", "cS", 2, 4, v("X"), "sU")
+            if t == 0:
+                cands(1, 0)
+            gather("V", "cS", 6, 8, v("X"), "sU")
+            decide()
+            if t == 0:
+                cands(1, 1)
+            dist("AB", "cS", "WTS", (4, 0, 5, 1, 6, 2, 7, 3))
+            if t == 0:
+                cands(1, 2)
+            values()
+            keys()
+            least("PLB", 8, 32)
+            turn(8, 15, 32, "PLB")
+            row(8, 32, "PLB")
+        sums("KEY", "AB", 0, "KBS", 0, 16, False)
+        sums("KEY", "AB", 1, "KBS", 1, 16, True)
+        vcopy(ind(v("HF"), v("nU", 16, 32)), v("HV"))
+        if last:
+            vcopy(ind(v("HF"), v("nU", 32, 48)), v("HV"))
+            store(T.yh[:, :], v("HF", 0, 2048), "o_h", 1)
+            store(T.yf[:, :], v("HF", 0, 2048), "o_f", 0)
+        else:
+            lists(8, 32, "ZA", mo)
+        least("KEY", 16, 0)
+        turn(16, 63, 0, "TR")
+        row(16, 0, "TR")
+        lists(16, 0, "ZL", so)
+        if not last:
+            ts(t1, mo, 2.0, A.mult, 1.0, A.add)
+            tt(t1, t1, v("QU%d" % t, 0, 16), A.mult)
+            tt(v("LI", 160, 176), t1, v("QU%d" % t, 16, 32), A.add)
+            ts(v("LI", 176, 192), v("LI", 160, 176), 4095, A.bitwise_and)
+            vcopy(v("qU"), v("LI", 176, 192))
+        aN = "aF%d" % (t + 1)
+        tt(t2, so, pop, A.mult)
+        tt(v(aN, 16, 32), t2, ak, A.add)
+        vcopy(v("aU%d" % (t + 1)), v(aN, 16, 32))
+        vcopy(v(aN, 32, 48), v(aN, 16, 32))
+        if t + 1 < STEPS - 1:
+            ask(t + 1)
+    vcopy(v("KU"), ind(v("IOT"), v("aU%d" % STEPS)))
+    store(T.ya[:, :], v("KU"), "o_a", 0)
+    g.wait_ge(T.sem.sent, sent[0])
+    for s, x in [("e" + q, cnt[q]) for q in cnt] + final:
+        if known["G"].get(s, 0) < x:
+            g.wait_ge(T.sem[s], x)

@@ -198,9 +198,7 @@ def rank_program(g, core, T, topo):
     (pF, pm, pg, g0, g1, g15, wi, wE, c1, p8, p31, w8) = [col(k) for k in range(12)]
 
     def cands(t, part):
-        z = "Z%d" % t
-        uv = "UV%d" % t
-        o = v("ML", 96, 112)
+        z, uv, o, r = "Z%d" % t, "UV%d" % t, v("ML", 96, 112), "TR"
         li = [v("LI", 16 * k, 16 * k + 16) for k in range(8)]
         if part == 0:
             for i in range(16):
@@ -215,14 +213,13 @@ def rank_program(g, core, T, topo):
             ts(li[6], li[4], 63, A.bitwise_and)
             ts(v("vhB"), li[5], 64.0, A.mult)
             vcopy(v("vlB"), li[6])
-            r = "TR"
             mm(v(r, 0, 256), v("WR1"), v(z), True, False)
             mm(v(r, 0, 256), v("WR2"), v(z), False, False)
             for i in range(16):
                 for b in ("vhB", "vlB"):
                     mm(v(r, i, 256, 16), v("Fa", 128 * i, 128 * i + 128), v(b), False, i == 15 and b == "vlB")
         if part == 2:
-            vcopy(v("TI"), v("TR", 0, 256))
+            vcopy(v("TI"), v(r, 0, 256))
             ts(v("TJ"), v("TI"), 4095, A.bitwise_and)
             vcopy(v("CL%d" % t), v("TJ"))
             q = (rank + 1 + t) % n
@@ -242,24 +239,25 @@ def rank_program(g, core, T, topo):
     ts(g15, pg, 16.0, A.mult, 15.0, A.add)
     ts(wi, pm, 2.0, A.mult, 1.0, A.add)
     ts(v("ZW"), v("JX"), g15, A.is_equal, wi, A.mult)
-    vcopy(v("aU0"), v("aI"))
-    ask(0)
-    cands(0, 0)
     ts(v("SG"), v("JG"), pg, A.is_equal)
     ts(v("OH"), v("J16"), pm, A.is_equal)
-    for r, w in (("RA", "WR1"), ("RB", "WR2")):
-        ts(v("W1"), v(r), wi, A.mult)
-        tt(v(w), v("W1"), v("SG"), A.mult)
+    cands(0, 0)
     for i in range(16):
-        ts(v("Fa", 128 * i, 128 * i + 128), v("SG"), v("OH", i, i + 1), A.mult)
-    cands(0, 1)
+        act(v("Fa", 128 * i, 128 * i + 128), v("SG"), scale=v("OH", i, i + 1))
+    vcopy(v("aU0"), v("aI"))
+    ask(0)
     ts(g0, pg, 16.0, A.mult)
     ts(g1, g0, 1.0, A.add)
     ts(v("SGf"), v("JX", 0, 128), g0, A.is_equal)
     ts(v("SGh"), v("JX", 0, 128), g1, A.is_equal)
+    ts(v("LT"), v("J16"), pm, A.is_gt)
     for i in range(16):
         act(v("Ff", 128 * i, 128 * i + 128), v("SGf"), scale=v("OH", i, i + 1))
         act(v("Fh", 128 * i, 128 * i + 128), v("SGh"), scale=v("OH", i, i + 1))
+    for r, w in (("RA", "WR1"), ("RB", "WR2")):
+        ts(v("W1"), v(r), wi, A.mult)
+        tt(v(w), v("W1"), v("SG"), A.mult)
+    cands(0, 1)
     cands(0, 2)
     vcopy(v("HB"), v("HI"))
     vcopy(v("FB"), v("FI"))
@@ -276,18 +274,17 @@ def rank_program(g, core, T, topo):
     fill(v("ZROW"), 0.0)
     fill(v("ZR16"), 0.0)
     fill(v("G", 4096, 4112), 0.0)
-    ts(v("LT"), v("J16"), pm, A.is_gt)
     tt(v("SGp"), v("SGf"), v("SGh"), A.add)
+    for i in range(1, 16):
+        act(v("LTm", 128 * i, 128 * i + 128), v("SGf"), scale=v("LT", i, i + 1))
 
     def late_constants():
-        for i in range(1, 16):
-            ts(v("LTm", 128 * i, 128 * i + 128), v("SGf"), v("LT", i, i + 1), A.mult)
         ts(wE, pm, 0.0, A.is_equal)
         ts(c1, pm, 1.0, A.is_equal, 512.0, A.mult)
         tt(wE, wE, c1, A.add)
         ts(v("ZE"), v("JX"), g15, A.is_equal, wE, A.mult)
         ts(v("mI"), v("JX", 0, 128), pF, A.is_equal)
-        ts(v("mNI"), v("mI"), -1.0, A.mult)
+        act(v("mNI"), v("mI"), scale=-1.0)
         ts(v("REP"), v("JR"), p31, A.is_equal)
         ts(v("JM"), v("JG"), -16.0, A.mult)
         tt(v("JM"), v("JM"), v("JX", 0, 128), A.add)
@@ -362,7 +359,7 @@ def rank_program(g, core, T, topo):
     for t in range(STEPS):
         last = t == STEPS - 1
         aF, aU, z, zn = "aF%d" % t, v("aU%d" % t), "Z%d" % t, "Z%d" % (t + 1)
-        aL, slot = v(aF, 16, 32), v(aF, 0, 16)
+        aL, slot, bank = v(aF, 16, 32), v(aF, 0, 16), v("G", 0, 4096)
         nn, ss, t1, segf, ask_, q1, n0, lf, pop, fm, ak, put, wA, n1 = [v("LL", 16 * x, 16 * x + 16) for x in range(14)]
         three, t2 = v("LL", 176, 224), v("LL", 240, 256)
         k, f, ct, hh, hs, hk = [v("LI", x, x + 16) for x in (224, 240, 256, 272, 128, 144)]
@@ -374,6 +371,12 @@ def rank_program(g, core, T, topo):
                 for b, w in (("shB", "PH"), ("slB", "PL")):
                     mm(v("KEY", h, 512, 2), v(b, 128 * h, 128 * h + 128), v(w), False, False)
             sums("KEY", "cS", 1, "KBS", 2, 16, False)
+
+        def ready():
+            terms("TR", zn, None)
+            vcopy(v("WTS"), v("TR", 0, 256))
+            mm(ro, v("SG"), v("scB"), True, False)
+            mm(ro, v("TRI"), v("blB"), False, True)
 
         def decide():
             ts(ask_, ro, 112.0, A.is_lt)
@@ -406,12 +409,6 @@ def rank_program(g, core, T, topo):
             act(v("HV"), v("TR", 0, 256))
 
         vcopy(v("AR"), ind(v("IOT"), aU))
-        vcopy(v("sI"), ind(v("SU"), aU))
-        vcopy(v("sU"), v("sI"))
-        if t:
-            vcopy(v("AN%d" % (t - 1)), ind(v("G", 0, 4096), v("qU")))
-            send((rank - t) % n, [(v("AN%d" % (t - 1)), "LN%d" % (t - 1), "r_n%d" % (t - 1))])
-        gather("S", "cS", 0, 2, v("X"), "sU")
         mm(v("PLB", 0, 256), v("ONE", p0=0, p1=1), v("ZROW", p0=0, p1=1), True, False)
         for c in range(16):
             e = 256 * c
@@ -419,27 +416,34 @@ def rank_program(g, core, T, topo):
             mm(v("PLB", 0, 16 * c + 16), v("SGh"), v("E", e, e + 16 * c + 16), False, False)
             if c < 15:
                 mm(v("PLB", 16 * c + 16, 256), v("SGp"), v("E", e + 16 * c + 16, e + 256), False, False)
+            if c == 1:
+                vcopy(v("sI"), ind(v("SU"), aU))
+                vcopy(v("sU"), v("sI"))
+                gather("S", "cS", 4, 8, v("X"), "sU")
         if t == 0:
             late_constants()
         for i in range(1, 16):
             mm(v("PLB", i, 256, 16), v("LTm", 128 * i, 128 * i + 128), v("E", i, 4096, 272), False, i == 15)
         act(v("RR", 0, 256), v("PLB", 0, 256))
-        if t:
-            vcopy(ind(v("HF"), v("nU", 32, 48)), v("HV"))
+        ts(v("sJ", 0, 256), v("sI"), 6, A.logical_shift_right)
+        ts(v("sJ", 256, 512), v("sI"), 63, A.bitwise_and)
+        vcopy(v("shB"), v("sJ", 0, 256))
+        vcopy(v("slB"), v("sJ", 256, 512))
         act(v("RR", 256, 512), ind(v("HF", 0, 2048), aU))
         for i in range(16):
             mm(o, v("ZE", 15 - i, 143 - i), v("RR", i, 512, 16), i == 0, i == 15)
         if t:
             vcopy(ind(v("G"), v("nU", 0, 16)), v("LN%d" % (t - 1)))
         if last:
-            gather("V", "cS", 6, 8, v("X"), "sU")
-            gather("S", "cS", 2, 6, v("X"), "sU")
+            gather("S", "cS", 0, 3, v("X"), "sU")
+            gather("V", "cS", 3, 4, v("X"), "sU")
         else:
-            gather("V", "cA", 4, 6, v("G", 0, 4096), "QC%d" % t)
             act(v("goal"), ind(v("X"), v("QA%d" % t)))
-            gather("S", "cA", 0, 4, v("G", 0, 4096), "QC%d" % t)
+            gather("S", "cA", 0, 4, bank, "QC%d" % t)
+            gather("V", "cA", 4, 8, bank, "QC%d" % t)
             terms("WTP", "goal", "QZ%d" % t)
-            gather("S", "cA", 6, 8, v("G", 0, 4096), "QC%d" % t)
+            ts(v("WTA"), v("WTP", 0, 256), -16.0, A.max, 16.0, A.min)
+        keys()
         vcopy(v("LI", 192, 224), o)
         ts(v("LI", 224, 256), v("LI", 192, 224), 511, A.bitwise_and)
         ts(v("LI", 256, 288), v("LI", 192, 224), 9, A.logical_shift_right)
@@ -454,65 +458,56 @@ def rank_program(g, core, T, topo):
         vcopy(v("gU"), segf)
         tt(v("zt"), ind(v("G", 0, 4112), v("gU")), v(z), A.add)
         ts(v(zn), v("zt"), 0.0, A.max, 255.0, A.min)
-        if not last:
-            ts(v("WTA"), v("WTP", 0, 256), -16.0, A.max, 16.0, A.min)
         op("V", lambda: g.vector.tensor_tensor_scan(out=ap(v("scB")), data0=ap(v("blB")), data1=ap(v("ZR16")), initial=0.0, op0=A.add, op1=A.add),
            v("scB"), v("blB"), v("ZR16"))
-        terms("TR", zn, None)
-        vcopy(v("WTS"), v("TR", 0, 256))
-        ts(v("sJ", 0, 256), v("sI"), 6, A.logical_shift_right)
-        ts(v("sJ", 256, 512), v("sI"), 63, A.bitwise_and)
-        vcopy(v("shB"), v("sJ", 0, 256))
-        vcopy(v("slB"), v("sJ", 256, 512))
-        mm(ro, v("SG"), v("scB"), True, False)
-        mm(ro, v("TRI"), v("blB"), False, True)
         if last:
             store(T.yz[:, :], v(zn), "o_z")
+            ready()
             decide()
-            dist("AB", "cS", "WTS", (4, 5, 0, 1, 2, 3, 6, 7))
-            values()
-            keys()
+            dist("AB", "cS", "WTS", (0, 1, 4, 2, 5, 3, 6, 7))
+            sums("KEY", "AB", 0, "KBS", 0, 16, False)
+            sums("KEY", "AB", 1, "KBS", 1, 16, True)
         else:
             mm(v("PLB", 0, 256), v("ONE", p0=0, p1=1), v("CRA", p0=0, p1=1), True, False)
-            dist("AC", "cA", "WTA", (4, 0, 5, 1, 6, 2, 7, 3))
             sums("PLB", "cA", 1, "KBA", 2, 8, False)
-            sums("PLB", "AC", 0, "KBA", 0, 8, False)
-            sums("PLB", "AC", 1, "KBA", 1, 8, True)
-            gather("S", "cS", 4, 6, v("X"), "sU")
-            gather("S", "cS", 2, 4, v("X"), "sU")
+            dist("AC", "cA", "WTA", (0, 4, 1, 5, 2, 3, 6, 7))
             if t == 0:
                 cands(1, 0)
-            gather("V", "cS", 6, 8, v("X"), "sU")
-            decide()
+            ready()
             if t == 0:
                 cands(1, 1)
-            dist("AB", "cS", "WTS", (4, 0, 5, 1, 6, 2, 7, 3))
+            gather("S", "cS", 0, 4, v("X"), "sU")
             if t == 0:
                 cands(1, 2)
+            sums("PLB", "AC", 0, "KBA", 0, 8, False)
+            sums("PLB", "AC", 1, "KBA", 1, 8, True)
+            decide()
+            dist("AB", "cS", "WTS", (4, 5))
             values()
-            keys()
+            dist("AB", "cS", "WTS", (0, 6, 1, 7, 2, 3))
+            vcopy(ind(v("HF"), v("nU", 16, 32)), v("HV"))
             least("PLB", 8, 32)
+            sums("KEY", "AB", 1, "KBS", 1, 16, False)
             turn(8, 15, 32, "PLB")
-            row(8, 32, "PLB")
-        sums("KEY", "AB", 0, "KBS", 0, 16, False)
-        sums("KEY", "AB", 1, "KBS", 1, 16, True)
-        vcopy(ind(v("HF"), v("nU", 16, 32)), v("HV"))
-        if last:
             vcopy(ind(v("HF"), v("nU", 32, 48)), v("HV"))
-            store(T.yh[:, :], v("HF", 0, 2048), "o_h", 1)
-            store(T.yf[:, :], v("HF", 0, 2048), "o_f", 0)
-        else:
+            row(8, 32, "PLB")
+            sums("KEY", "AB", 0, "KBS", 0, 16, True)
             lists(8, 32, "ZA", mo)
         least("KEY", 16, 0)
         turn(16, 63, 0, "TR")
-        row(16, 0, "TR")
-        lists(16, 0, "ZL", so)
         if not last:
             ts(t1, mo, 2.0, A.mult, 1.0, A.add)
             tt(t1, t1, v("QU%d" % t, 0, 16), A.mult)
             tt(v("LI", 160, 176), t1, v("QU%d" % t, 16, 32), A.add)
             ts(v("LI", 176, 192), v("LI", 160, 176), 4095, A.bitwise_and)
             vcopy(v("qU"), v("LI", 176, 192))
+            vcopy(v("AN%d" % t), ind(bank, v("qU")))
+            send((rank - 1 - t) % n, [(v("AN%d" % t), "LN%d" % t, "r_n%d" % t)])
+        row(16, 0, "TR")
+        lists(16, 0, "ZL", so)
+        if last:
+            values()
+            vcopy(ind(v("HF"), v("nU", 16, 32)), v("HV"))
         aN = "aF%d" % (t + 1)
         tt(t2, so, pop, A.mult)
         tt(v(aN, 16, 32), t2, ak, A.add)
@@ -522,6 +517,9 @@ def rank_program(g, core, T, topo):
             ask(t + 1)
     vcopy(v("KU"), ind(v("IOT"), v("aU%d" % STEPS)))
     store(T.ya[:, :], v("KU"), "o_a", 0)
+    vcopy(ind(v("HF"), v("nU", 32, 48)), v("HV"))
+    store(T.yh[:, :], v("HF", 0, 2048), "o_h", 1)
+    store(T.yf[:, :], v("HF", 0, 2048), "o_f", 0)
     g.wait_ge(T.sem.sent, sent[0])
     for s, x in [("e" + q, cnt[q]) for q in cnt] + final:
         if known["G"].get(s, 0) < x:

from concourse.bass import DstId, RemoteDMATransfer
from concourse.mybir import AluOpType as A, ActivationFunctionType as F

SCRATCH = {}


def _b(n, c, d="bfloat16", w="sbuf", p=128):
    SCRATCH[n] = (w, [p, c], d)


for _n, _c in (("X", 2048), ("G", 4368), ("FB", 128), ("HB", 128), ("cS", 4096), ("cA", 4096), ("AB", 4096), ("AC", 4096),
               ("E", 4096), ("mI", 128), ("mNI", 128), ("SG", 128), ("SGf", 128), ("SGh", 128), ("SGp", 128), ("ZE", 144),
               ("ZW", 144), ("ZL", 144), ("ZA", 144), ("TRI", 128), ("Fa", 2048), ("Ff", 2048), ("Fh", 2048), ("LTm", 2048),
               ("WR1", 128), ("WR2", 128), ("REP", 512), ("KBS", 48), ("KBA", 24), ("PH", 256), ("PL", 256), ("ONE", 128),
               ("CRS", 512), ("CRA", 256), ("ZROW", 256), ("RR", 512), ("blB", 16), ("scB", 16), ("hpB", 16), ("fpB", 16),
               ("vhB", 16), ("vlB", 16), ("shB", 256), ("slB", 256), ("zt", 256), ("WTS", 256), ("WTA", 256), ("goal", 256),
               ("PB", 48), ("T16", 512), ("Z0", 256), ("Z1", 256), ("Z2", 256), ("Z3", 256), ("AN0", 256), ("AN1", 256),
               ("LN0", 256), ("LN1", 256), ("QZ0", 256), ("QZ1", 256)):
    _b(_n, _c)
for _n, _c in (("HF", 2304), ("JX", 144), ("JG", 128), ("JM", 128), ("JPH", 256), ("JPL", 256), ("JR", 512), ("RA", 128),
               ("RB", 128), ("J16", 16), ("KB2", 16), ("COL", 128), ("OH", 16), ("LT", 16), ("LA", 48), ("W1", 128),
               ("ZR16", 16), ("LL", 512), ("KU", 256), ("K1", 256), ("K2", 128), ("K3", 64), ("HV", 256),
               ("aF0", 48), ("aF1", 48), ("aF2", 48), ("aF3", 48), ("UV0", 32), ("UV1", 32), ("QU0", 32), ("QU1", 32)):
    _b(_n, _c, "float32")
for _n, _c in (("SU", 2048), ("IOT", 2048), ("FI", 128), ("HI", 128), ("aI", 16), ("CI", 8), ("LI", 320), ("TI", 256), ("TJ", 256),
               ("sI", 256), ("sJ", 512), ("KI", 48), ("KJ", 48)):
    _b(_n, _c, "int32")
for _n, _c in (("aU0", 16), ("aU1", 16), ("aU2", 16), ("aU3", 16), ("AR", 256), ("sU", 256), ("gU", 16), ("nU", 48),
               ("qU", 16), ("CL0", 256), ("CL1", 256), ("QC0", 256), ("QC1", 256), ("QA0", 16), ("QA1", 16)):
    _b(_n, _c, "uint16")
for _n in ("D0", "D1", "D2", "KEY", "PLB", "ML", "WTP", "TR"):
    _b(_n, 512, "float32", "psum")
SEMAPHORES = ["eV", "eS", "eP", "eG", "sent", "l_a", "l_z", "l_h", "l_f", "l_s", "l_x", "l_g", "o_z", "o_a", "o_h", "o_f",
              "r_z0", "r_z1", "r_c0", "r_c1", "r_u0", "r_u1", "r_a0", "r_a1", "r_n0", "r_n1"]
STEPS = 3


def rank_program(g, core, T, topo):
    rank = T.rank_of(core)
    if rank is None:
        return
    n = len(T.cores)
    H = {"V": g.vector, "S": g.scalar, "P": g.tensor, "G": g, "Y": g.sync}
    cnt = {"V": 0, "S": 0, "P": 0, "G": 0}
    known = {q: {} for q in H}
    wr, rd, pacc = {}, {}, {}

    def v(name, c0=0, c1=None, st=1, p0=0, p1=None):
        sh = SCRATCH[name][1]
        return (name, c0, sh[1] if c1 is None else c1, st, p0, sh[0] if p1 is None else p1)

    def ap(x):
        if not isinstance(x, tuple):
            return x
        if x[0] == "ind":
            return ap(x[1]).indirect(ap(x[2]))
        name, c0, c1, st, p0, p1 = x
        return T[name][p0:p1, c0:c1] if st == 1 else T[name][p0:p1, c0:c1:st]

    def ind(win, off):
        return ("ind", win, off)

    def wait(q, rec):
        sem, val, kn = rec[1], rec[2], rec[3]
        if known[q].get(sem, 0) >= val:
            return
        H[q].wait_ge(T.sem[sem], val)
        for s, x in list(kn.items()) + [(sem, val)]:
            if known[q].get(s, 0) < x:
                known[q][s] = x

    def flat(xs):
        out = []
        for x in xs:
            if isinstance(x, tuple):
                out += [x[1], x[2]] if x[0] == "ind" else [x]
        return out

    def deps(q, ws, rs):
        need = []
        for x in ws + rs:
            if SCRATCH[x[0]][0] == "psum":
                need += [r for k, r in pacc.get(x[0], {}).items() if k != q]
            need += [r for lo, hi, r in wr.get(x[0], []) if lo < x[2] and x[1] < hi]
        for x in ws:
            need += [r for lo, hi, r in rd.get(x[0], []) if lo < x[2] and x[1] < hi]
        for r in sorted(need, key=lambda r: -r[2]):
            wait(q, r)

    def note(rec, ws, rs, cover=True):
        for x in ws + rs:
            if SCRATCH[x[0]][0] == "psum":
                pacc.setdefault(x[0], {})[rec[0]] = rec
        for x in ws:
            if SCRATCH[x[0]][0] == "psum":
                continue
            if x[3] == 1 and cover:
                wr[x[0]] = [e for e in wr.get(x[0], []) if not (x[1] <= e[0] and e[1] <= x[2])]
                rd[x[0]] = [e for e in rd.get(x[0], []) if not (x[1] <= e[0] and e[1] <= x[2])]
            wr.setdefault(x[0], []).append((x[1], x[2], rec))
        for x in rs:
            if SCRATCH[x[0]][0] != "psum":
                rd[x[0]] = [e for e in rd.get(x[0], []) if not (e[2][0] == rec[0] and not e[2][4] and x[1] <= e[0] and e[1] <= x[2])]
                rd[x[0]].append((x[1], x[2], rec))

    def op(q, call, out, *ins):
        ws, rs = flat([out]), flat(ins)
        if out[0] == "ind":
            ws, rs = [out[1]], rs + [out[2]]
        deps(q, ws, rs)
        cnt[q] += 1
        call().then_inc(T.sem["e" + q], 1)
        note((q, "e" + q, cnt[q], dict(known[q]), False), ws, rs, out[0] != "ind")

    def vcopy(out, in_):
        op("V", lambda: g.vector.tensor_copy(out=ap(out), in_=ap(in_)), out, in_)

    def tt(out, a, b, o):
        op("V", lambda: g.vector.tensor_tensor(out=ap(out), in0=ap(a), in1=ap(b), op=o), out, a, b)

    def ts(out, a, s1, o1, s2=None, o2=None):
        if o2 is None:
            op("V", lambda: g.vector.tensor_scalar(out=ap(out), in0=ap(a), scalar1=ap(s1), scalar2=None, op0=o1), out, a, s1)
        else:
            op("V", lambda: g.vector.tensor_scalar(out=ap(out), in0=ap(a), scalar1=ap(s1), scalar2=ap(s2), op0=o1, op1=o2), out, a, s1, s2)

    def act(out, in_, f=F.Copy, scale=1.0):
        op("S", lambda: g.scalar.activation(out=ap(out), in_=ap(in_), func=f, scale=ap(scale)), out, in_, scale)

    def mm(out, lhsT, rhs, start, stop):
        op("P", lambda: g.tensor.matmul(ap(out), ap(lhsT), ap(rhs), start, stop), out, lhsT, rhs)

    def iota(out, pat, base=0, mult=0):
        op("G", lambda: g.iota(ap(out), pat, base, mult, allow_small_or_imprecise_dtypes=True), out)

    def fill(out, x):
        op("V", lambda: g.vector.memset(ap(out), x), out)

    def load(q, out, in_, sem):
        H[q].dma_start(out=ap(out), in_=in_).then_inc(T.sem[sem], 16)
        note((q, sem, 16, {}, True), [out], [])

    final, sent = [], [0]

    def store(out, in_, sem, row=None):
        deps("Y", [], [in_])
        src = ap(in_) if row is None else T[in_[0]][row:128:16, in_[1]:in_[2]]
        g.sync.dma_start(out=out, in_=src).then_inc(T.sem[sem], 16)
        final.append((sem, 16))

    def send(dst, parts):
        to = T.cores[dst]
        rid, pid = topo.addr(to)[0], topo.addr(to)[1]
        e = topo.engines(core, to)[:8]
        deps("G", [], [p[0] for p in parts])
        m = [sum(1 << x for x in e[k::len(parts)]) for k in range(len(parts))]
        sent[0] += len(e)
        if len(parts) == 1:
            s, d, sem = parts[0]
            g.remote_dma(ap(v(d)), ap(s), T.sem[sem], T.sem.sent, pid, rid, m[0])
        else:
            g.remote_dma_fused([RemoteDMATransfer(dst_ids=[DstId(rid=rid, pnc=pid)], dma_engine_mask=m[k], remote_sem=T.sem[sem],
                                                  src=ap(s), dst=ap(v(d))) for k, (s, d, sem) in enumerate(parts)], local_sem=T.sem.sent)

    def arrive(buf, sem, src, parts):
        e = len(topo.engines(T.cores[src], core)[:8]) // parts
        wr[buf] = [(0, SCRATCH[buf][1][1], ("R", sem, e, {}, True))]

    load("Y", v("aI"), T.a0[:, :], "l_a")
    load("S", v("Z0"), T.z0[:, :], "l_z")
    load("Y", v("SU"), T.su[:, :], "l_s")
    load("S", v("HI"), T.hd0[:, :], "l_h")
    load("S", v("FI"), T.fl0[:, :], "l_f")
    load("Y", v("X"), T.xs[:, :], "l_x")
    load("S", v("G", 0, 4096), T.gs[:, :], "l_g")
    for t in range(2):
        p, q = (rank - 1 - t) % n, (rank + 1 + t) % n
        for b, c in (("QZ", 2), ("QC", 2), ("QU", 1), ("QA", 1)):
            arrive(b + str(t), "r_" + b[1].lower() + str(t), p, c)
        arrive("LN%d" % t, "r_n%d" % t, q, 1)

    iota(v("CI", 0, 1), [[0, 1]], 0, 1)
    iota(v("JX"), [[1, 144]])
    iota(v("J16"), [[1, 16]])
    iota(v("JG"), [[1, 8], [0, 16]])
    iota(v("RA"), [[0, 8], [8, 4], [0, 4]])
    iota(v("RB"), [[0, 32], [2, 4]], 1)
    iota(v("IOT"), [[1, 2048]])
    iota(v("JR"), [[1, 32], [0, 16]])
    iota(v("KB2"), [[0, 2], [1, 8]])
    iota(v("CRA", p0=0, p1=1), [[1, 16], [0, 16]])
    iota(v("CRS", p0=0, p1=1), [[64, 16], [0, 32]])
    iota(v("JPH"), [[1, 16], [1000, 2], [16, 8]])
    iota(v("JPL"), [[1, 16], [1000, 2], [16, 8]], -1000)

    def col(k):
        return v("COL", 4 * k, 4 * k + 1)
    (pF, pm, pg, g0, g1, g15, wi, wE, c1, p8, p31, w8) = [col(k) for k in range(12)]

    def cands(t, part):
        z, uv, o, r = "Z%d" % t, "UV%d" % t, v("ML", 96, 112), "TR"
        li = [v("LI", 16 * k, 16 * k + 16) for k in range(8)]
        if part == 0:
            for i in range(16):
                mm(o, v("ZW", 15 - i, 143 - i), v(z, i, 256, 16), i == 0, i == 15)
        if part == 1:
            vcopy(li[0], o)
            ts(li[1], li[0], 4095, A.bitwise_and)
            tt(li[2], li[1], li[1], A.mult)
            ts(li[3], li[2], 5, A.logical_shift_right)
            ts(li[4], li[3], 4095, A.bitwise_and)
            ts(li[5], li[4], 6, A.logical_shift_right)
            ts(li[6], li[4], 63, A.bitwise_and)
            ts(v("vhB"), li[5], 64.0, A.mult)
            vcopy(v("vlB"), li[6])
            mm(v(r, 0, 256), v("WR1"), v(z), True, False)
            mm(v(r, 0, 256), v("WR2"), v(z), False, False)
            for i in range(16):
                for b in ("vhB", "vlB"):
                    mm(v(r, i, 256, 16), v("Fa", 128 * i, 128 * i + 128), v(b), False, i == 15 and b == "vlB")
        if part == 2:
            vcopy(v("TI"), v(r, 0, 256))
            ts(v("TJ"), v("TI"), 4095, A.bitwise_and)
            vcopy(v("CL%d" % t), v("TJ"))
            q = (rank + 1 + t) % n
            send(q, [(v(z), "QZ%d" % t, "r_z%d" % t), (v("CL%d" % t), "QC%d" % t, "r_c%d" % t)])
            vcopy(v(uv, 0, 16), li[1])
            vcopy(v(uv, 16, 32), li[4])
            send(q, [(v(uv), "QU%d" % t, "r_u%d" % t)])

    def ask(t):
        send((rank + 1 + t) % n, [(v("aU%d" % t), "QA%d" % t, "r_a%d" % t)])

    vcopy(pF, v("CI", 0, 1))
    for j, (out, o, s) in enumerate(((pm, A.bitwise_and, 15), (pg, A.logical_shift_right, 4), (p8, A.bitwise_and, 7),
                                     (p31, A.bitwise_and, 31))):
        ts(v("CI", 1 + j, 2 + j), v("CI", 0, 1), s, o)
        vcopy(out, v("CI", 1 + j, 2 + j))
    ts(g15, pg, 16.0, A.mult, 15.0, A.add)
    ts(wi, pm, 2.0, A.mult, 1.0, A.add)
    ts(v("ZW"), v("JX"), g15, A.is_equal, wi, A.mult)
    ts(v("SG"), v("JG"), pg, A.is_equal)
    ts(v("OH"), v("J16"), pm, A.is_equal)
    cands(0, 0)
    for i in range(16):
        act(v("Fa", 128 * i, 128 * i + 128), v("SG"), scale=v("OH", i, i + 1))
    vcopy(v("aU0"), v("aI"))
    ask(0)
    ts(g0, pg, 16.0, A.mult)
    ts(g1, g0, 1.0, A.add)
    ts(v("SGf"), v("JX", 0, 128), g0, A.is_equal)
    ts(v("SGh"), v("JX", 0, 128), g1, A.is_equal)
    ts(v("LT"), v("J16"), pm, A.is_gt)
    for i in range(16):
        act(v("Ff", 128 * i, 128 * i + 128), v("SGf"), scale=v("OH", i, i + 1))
        act(v("Fh", 128 * i, 128 * i + 128), v("SGh"), scale=v("OH", i, i + 1))
    for r, w in (("RA", "WR1"), ("RB", "WR2")):
        ts(v("W1"), v(r), wi, A.mult)
        tt(v(w), v("W1"), v("SG"), A.mult)
    cands(0, 1)
    cands(0, 2)
    vcopy(v("HB"), v("HI"))
    vcopy(v("FB"), v("FI"))
    for b in range(4):
        d = "D%d" % (b % 3)
        for k in range(4):
            i = 4 * b + k
            mm(v(d, 128 * k, 128 * k + 128), v("Ff", 128 * i, 128 * i + 128), v("FB"), True, False)
            mm(v(d, 128 * k, 128 * k + 128), v("Fh", 128 * i, 128 * i + 128), v("HB"), False, True)
        act(v("HF", 512 * b, 512 * b + 512), v(d))
    vcopy(v("aF0", 16, 32), v("aI"))
    vcopy(v("aF0", 32, 48), v("aI"))
    fill(v("ONE"), 1.0)
    fill(v("ZROW"), 0.0)
    fill(v("ZR16"), 0.0)
    fill(v("G", 4096, 4112), 0.0)
    tt(v("SGp"), v("SGf"), v("SGh"), A.add)
    for i in range(1, 16):
        act(v("LTm", 128 * i, 128 * i + 128), v("SGf"), scale=v("LT", i, i + 1))

    def late_constants():
        ts(wE, pm, 0.0, A.is_equal)
        ts(c1, pm, 1.0, A.is_equal, 512.0, A.mult)
        tt(wE, wE, c1, A.add)
        ts(v("ZE"), v("JX"), g15, A.is_equal, wE, A.mult)
        ts(v("mI"), v("JX", 0, 128), pF, A.is_equal)
        act(v("mNI"), v("mI"), scale=-1.0)
        ts(v("REP"), v("JR"), p31, A.is_equal)
        ts(v("JM"), v("JG"), -16.0, A.mult)
        tt(v("JM"), v("JM"), v("JX", 0, 128), A.add)
        ts(v("W1"), v("JM"), pm, A.is_gt)
        tt(v("TRI"), v("W1"), v("SG"), A.mult)
        tt(v("TRI"), v("TRI"), v("SG"), A.subtract)
        ts(v("LA", 0, 16), v("J16"), 16.0, A.mult, 4112.0, A.add)
        ts(v("LA", 0, 16), v("LA", 0, 16), pm, A.add)
        ts(v("LA", 16, 32), v("LA", 0, 16), -2064.0, A.add)
        ts(v("LA", 32, 48), v("LA", 0, 16), -2064.0, A.add)
        for k, f in enumerate((1.0, 2.0, -1.0)):
            ts(v("KBA", 8 * k, 8 * k + 8), v("KB2", 0, 8), pg, A.is_equal, 16.0 * f, A.mult)
            ts(v("KBS", 16 * k, 16 * k + 16), v("KB2"), pg, A.is_equal, 1024.0 * f, A.mult)
        ts(c1, p8, 16.0, A.mult, 15.0, A.add)
        ts(v("ZA"), v("JX"), c1, A.is_equal)
        ts(w8, pF, 8.0, A.is_lt, 63.0, A.mult)
        ts(w8, w8, 1.0, A.add)
        ts(v("ZL"), v("ZA"), w8, A.mult)
        ts(v("PH"), v("JPH"), pF, A.is_equal)
        ts(v("PL"), v("JPL"), pF, A.is_equal)

    def gather(q, out, k0, k1, win, lst):
        o, i = v(out, 512 * k0, 512 * k1), ind(win, v(lst, 32 * k0, 32 * k1))
        vcopy(o, i) if q == "V" else act(o, i)

    def terms(bank, pos, neg):
        for h in range(2):
            o, s = v(bank, 128 * h, 128 * h + 128), (128 * h, 128 * h + 128)
            mm(o, v(pos, *s), v("mI"), True, not neg)
            if neg:
                mm(o, v(neg, *s), v("mNI"), False, True)

    def dist(ab, src, term, order):
        for k in order:
            h, r = k // 4, 32 * (k % 4)
            d = v(("D0", "D1")[k % 2] if h == 0 else ("D2", "WTP")[k % 2])
            s, o = v(src, 512 * k, 512 * k + 512), v(ab, 512 * k, 512 * k + 512)
            if h == 0:
                mm(d, v("mNI"), s, True, False)
            mm(d, v(term, 128 * h, 128 * h + 128, 1, r, r + 32), v("REP", p0=r, p1=r + 32), h == 1, True)
            if h == 0:
                act(o, d, F.Abs)
            else:
                tt(o, s, d, A.max)

    def sums(bank, src, h, kb, k, w, last):
        for m in range(16):
            mm(v(bank, m * 2 * w + h, (m + 1) * 2 * w, 2), v(src, m + 2048 * h, 2048 * h + 2048, 16), v(kb, k * w, k * w + w), False,
               last and m == 15)

    def least(bank, w, k0):
        u = 16 * w
        vcopy(v("KU", 0, u), v(bank, u, 2 * u))
        tt(v("K1", 0, u), v(bank, 0, u), v("KU", 0, u), A.min)
        tt(v("K2", 0, u // 2), v("K1", 0, u // 2), v("K1", u // 2, u), A.min)
        tt(v("K3", 0, u // 4), v("K2", 0, u // 4), v("K2", u // 4, u // 2), A.min)
        tt(v("KI", k0, k0 + u // 8), v("K3", 0, u // 8), v("K3", u // 8, u // 4), A.min)

    def turn(w, mask, k0, bank):
        ts(v("KJ", k0, k0 + 2 * w), v("KI", k0, k0 + 2 * w), mask, A.bitwise_and)
        vcopy(v("PB", k0, k0 + 2 * w), v("KJ", k0, k0 + 2 * w))
        for h in range(2):
            mm(v(bank, 256 + 128 * h, 384 + 128 * h, 1, 0, w), v("PB", k0 + h, k0 + 2 * w, 2), v("mI"), True, True)

    def row(w, k0, bank):
        vcopy(v("T16", 8 * k0, 8 * k0 + 256, 1, 0, w), v(bank, 256, 512, 1, 0, w))

    def lists(w, k0, zs, o):
        for i in range(16):
            mm(o, v(zs, 15 - i, 143 - i, 1, 0, w), v("T16", 8 * k0 + i, 8 * k0 + 256, 16, 0, w), i == 0, i == 15)

    for t in range(STEPS):
        last = t == STEPS - 1
        aF, aU, z, zn = "aF%d" % t, v("aU%d" % t), "Z%d" % t, "Z%d" % (t + 1)
        aL, slot, bank = v(aF, 16, 32), v(aF, 0, 16), v("G", 0, 4096)
        nn, ss, t1, segf, ask_, q1, n0, lf, pop, fm, ak, put, wA, n1 = [v("LL", 16 * x, 16 * x + 16) for x in range(14)]
        three, t2 = v("LL", 176, 224), v("LL", 240, 256)
        k, f, ct, hh, hs, hk = [v("LI", x, x + 16) for x in (224, 240, 256, 272, 128, 144)]
        o, ro, mo, so = v("ML", 0, 32), v("ML", 64, 80), v("ML", 160, 176), v("ML", 128, 144)

        def keys():
            mm(v("KEY"), v("ONE", p0=0, p1=1), v("CRS", p0=0, p1=1), True, False)
            for h in range(2):
                for b, w in (("shB", "PH"), ("slB", "PL")):
                    mm(v("KEY", h, 512, 2), v(b, 128 * h, 128 * h + 128), v(w), False, False)
            sums("KEY", "cS", 1, "KBS", 2, 16, False)

        def ready():
            terms("TR", zn, None)
            vcopy(v("WTS"), v("TR", 0, 256))
            mm(ro, v("SG"), v("scB"), True, False)
            mm(ro, v("TRI"), v("blB"), False, True)

        def decide():
            ts(ask_, ro, 112.0, A.is_lt)
            ts(pop, v("blB"), -1.0, A.mult, 1.0, A.add)
            ts(q1, nn, 1.0, A.is_le)
            ts(t1, nn, 1.0, A.add)
            ts(n0, nn, 0.0, A.is_equal)
            tt(ask_, ask_, v("blB"), A.mult)
            ts(t2, nn, -1.0, A.mult, -1.0, A.add)
            tt(lf, ct, k, A.subtract)
            tt(fm, t1, ask_, A.mult)
            tt(v("hpB"), n0, hk, A.is_equal)
            tt(v("fpB"), t2, fm, A.max)
            ts(lf, lf, 1.0, A.is_equal)
            tt(put, q1, ask_, A.mult)
            ts(n1, nn, 1.0, A.is_equal)
            tt(lf, lf, pop, A.mult)
            tt(ak, aL, v("blB"), A.mult)
            tt(wA, n0, lf, A.max)
            tt(n1, n1, ask_, A.mult)
            ts(three, three, -1.0, A.mult, 1.0, A.add)
            tt(three, three, v("LA"), A.mult)
            tt(three, three, v(aF), A.max)
            vcopy(v("nU"), three)

        def values():
            for i in range(16):
                mm(v("TR", i, 256, 16), v("Ff", 128 * i, 128 * i + 128), v("fpB"), True, False)
                mm(v("TR", i, 256, 16), v("Fh", 128 * i, 128 * i + 128), v("hpB"), False, True)
            act(v("HV"), v("TR", 0, 256))

        vcopy(v("AR"), ind(v("IOT"), aU))
        mm(v("PLB", 0, 256), v("ONE", p0=0, p1=1), v("ZROW", p0=0, p1=1), True, False)
        for c in range(16):
            e = 256 * c
            ts(v("E", e, e + 256), v("AR"), v(aF, 16 + c, 17 + c), A.is_equal)
            mm(v("PLB", 0, 16 * c + 16), v("SGh"), v("E", e, e + 16 * c + 16), False, False)
            if c < 15:
                mm(v("PLB", 16 * c + 16, 256), v("SGp"), v("E", e + 16 * c + 16, e + 256), False, False)
            if c == 1:
                vcopy(v("sI"), ind(v("SU"), aU))
                vcopy(v("sU"), v("sI"))
                gather("S", "cS", 4, 8, v("X"), "sU")
        if t == 0:
            late_constants()
        for i in range(1, 16):
            mm(v("PLB", i, 256, 16), v("LTm", 128 * i, 128 * i + 128), v("E", i, 4096, 272), False, i == 15)
        act(v("RR", 0, 256), v("PLB", 0, 256))
        ts(v("sJ", 0, 256), v("sI"), 6, A.logical_shift_right)
        ts(v("sJ", 256, 512), v("sI"), 63, A.bitwise_and)
        vcopy(v("shB"), v("sJ", 0, 256))
        vcopy(v("slB"), v("sJ", 256, 512))
        act(v("RR", 256, 512), ind(v("HF", 0, 2048), aU))
        for i in range(16):
            mm(o, v("ZE", 15 - i, 143 - i), v("RR", i, 512, 16), i == 0, i == 15)
        if t:
            vcopy(ind(v("G"), v("nU", 0, 16)), v("LN%d" % (t - 1)))
        if last:
            gather("S", "cS", 0, 3, v("X"), "sU")
            gather("V", "cS", 3, 4, v("X"), "sU")
        else:
            act(v("goal"), ind(v("X"), v("QA%d" % t)))
            gather("S", "cA", 0, 4, bank, "QC%d" % t)
            gather("V", "cA", 4, 8, bank, "QC%d" % t)
            terms("WTP", "goal", "QZ%d" % t)
            ts(v("WTA"), v("WTP", 0, 256), -16.0, A.max, 16.0, A.min)
        keys()
        vcopy(v("LI", 192, 224), o)
        ts(v("LI", 224, 256), v("LI", 192, 224), 511, A.bitwise_and)
        ts(v("LI", 256, 288), v("LI", 192, 224), 9, A.logical_shift_right)
        tt(nn, k, f, A.subtract)
        tt(hs, hh, k, A.add)
        ts(v("blB"), nn, 0.0, A.is_ge)
        ts(hk, hs, 1, A.bitwise_and)
        ts(ss, aL, 2.0, A.mult)
        ts(t1, v("blB"), 4096.0, A.mult)
        tt(slot, ss, hk, A.add)
        tt(segf, t1, slot, A.max)
        vcopy(v("gU"), segf)
        tt(v("zt"), ind(v("G", 0, 4112), v("gU")), v(z), A.add)
        ts(v(zn), v("zt"), 0.0, A.max, 255.0, A.min)
        op("V", lambda: g.vector.tensor_tensor_scan(out=ap(v("scB")), data0=ap(v("blB")), data1=ap(v("ZR16")), initial=0.0, op0=A.add, op1=A.add),
           v("scB"), v("blB"), v("ZR16"))
        if last:
            store(T.yz[:, :], v(zn), "o_z")
            ready()
            decide()
            dist("AB", "cS", "WTS", (0, 1, 4, 2, 5, 3, 6, 7))
            sums("KEY", "AB", 0, "KBS", 0, 16, False)
            sums("KEY", "AB", 1, "KBS", 1, 16, True)
        else:
            mm(v("PLB", 0, 256), v("ONE", p0=0, p1=1), v("CRA", p0=0, p1=1), True, False)
            sums("PLB", "cA", 1, "KBA", 2, 8, False)
            dist("AC", "cA", "WTA", (0, 4, 1, 5, 2, 3, 6, 7))
            if t == 0:
                cands(1, 0)
            ready()
            if t == 0:
                cands(1, 1)
            gather("S", "cS", 0, 4, v("X"), "sU")
            if t == 0:
                cands(1, 2)
            sums("PLB", "AC", 0, "KBA", 0, 8, False)
            sums("PLB", "AC", 1, "KBA", 1, 8, True)
            decide()
            dist("AB", "cS", "WTS", (4, 5))
            values()
            dist("AB", "cS", "WTS", (0, 6, 1, 7, 2, 3))
            vcopy(ind(v("HF"), v("nU", 16, 32)), v("HV"))
            least("PLB", 8, 32)
            sums("KEY", "AB", 1, "KBS", 1, 16, False)
            turn(8, 15, 32, "PLB")
            vcopy(ind(v("HF"), v("nU", 32, 48)), v("HV"))
            row(8, 32, "PLB")
            sums("KEY", "AB", 0, "KBS", 0, 16, True)
            lists(8, 32, "ZA", mo)
        least("KEY", 16, 0)
        turn(16, 63, 0, "TR")
        if not last:
            ts(t1, mo, 2.0, A.mult, 1.0, A.add)
            tt(t1, t1, v("QU%d" % t, 0, 16), A.mult)
            tt(v("LI", 160, 176), t1, v("QU%d" % t, 16, 32), A.add)
            ts(v("LI", 176, 192), v("LI", 160, 176), 4095, A.bitwise_and)
            vcopy(v("qU"), v("LI", 176, 192))
            vcopy(v("AN%d" % t), ind(bank, v("qU")))
            send((rank - 1 - t) % n, [(v("AN%d" % t), "LN%d" % t, "r_n%d" % t)])
        row(16, 0, "TR")
        lists(16, 0, "ZL", so)
        if last:
            values()
            vcopy(ind(v("HF"), v("nU", 16, 32)), v("HV"))
        aN = "aF%d" % (t + 1)
        tt(t2, so, pop, A.mult)
        tt(v(aN, 16, 32), t2, ak, A.add)
        vcopy(v("aU%d" % (t + 1)), v(aN, 16, 32))
        vcopy(v(aN, 32, 48), v(aN, 16, 32))
        if t + 1 < STEPS - 1:
            ask(t + 1)
    vcopy(v("KU"), ind(v("IOT"), v("aU%d" % STEPS)))
    store(T.ya[:, :], v("KU"), "o_a", 0)
    vcopy(ind(v("HF"), v("nU", 32, 48)), v("HV"))
    store(T.yh[:, :], v("HF", 0, 2048), "o_h", 1)
    store(T.yf[:, :], v("HF", 0, 2048), "o_f", 0)
    g.wait_ge(T.sem.sent, sent[0])
    for s, x in [("e" + q, cnt[q]) for q in cnt] + final:
        if known["G"].get(s, 0) < x:
            g.wait_ge(T.sem[s], x)
